import numpy as np, ml_dtypes
CORES = [5,29,101,125,133,157,229,253]
N = 8
BF = ml_dtypes.bfloat16
def gentries(a):
    return np.ascontiguousarray(a.reshape(8, 16, -1).transpose(0, 2, 1)).reshape(8, -1)
def gtable(e):
    e = np.asarray(e); return np.ascontiguousarray(e.reshape(8, -1, 16).transpose(0, 2, 1)).reshape(128, -1).astype(np.int32)
I, L, S, T, H, R = 2560, 256, 4, 3, 13, 3
M = L // S
W = I + R * (L + M)
def pack(F, sel, P):
    return {"front": np.ascontiguousarray(F.reshape(N, 128, I)).astype(np.float32).astype(BF), "sel0": np.ascontiguousarray(sel).astype(np.int32), "par": np.stack([gtable(a.reshape(8, -1)) for a in P])}
def rows8(rng):
    return (np.argsort(rng.random((8, 16)), axis=1) < 8)[None, :, :, None]
def of_class(rng, cl, want, n):
    order = np.argsort(cl + 0.5 * rng.random(cl.shape), axis=-1)
    cnt = np.stack([np.add.reduce((cl == c).astype(np.int64), axis=-1) for c in range(n)], axis=-1)
    first = np.add.accumulate(cnt, axis=-1) - cnt; w = want.reshape(N, 8, -1)
    at = np.take_along_axis(first, w, 2) + (np.take_along_axis(cnt, w, 2) * rng.random(w.shape)).astype(np.int64)
    return np.take_along_axis(order, np.minimum(at, I - 1), 2).reshape(want.shape)
def setup_inputs(rng):
    hi = rows8(rng); share = rng.choice(np.array([0.06, 0.12, 0.2]), (N, 8, 1))
    cl = np.where(rng.random((N, 8, I)) < share, 0, 1 + rng.integers(0, 2, (N, 8, I)))
    u = rng.random((N, 8, 16, I)); c = cl[:, :, None, :]
    F = np.where((c > 0) & ((c == 1) == hi), 128 + 128 * u, np.where(c == 0, 64 * u, 101 * u)).astype(np.int64)
    y = rng.random((N, 8, I)); sel = of_class(rng, cl, np.where((cl == 0) | (y < 0.15), 0, np.where(y < 0.2, 3 - cl, cl)), 3)
    free = rng.permutation(8) < 2; F = np.where(free[None, :, None, None], (256 * u).astype(np.int64), F)
    return pack(F, sel, rng.integers(0, I, (N, 8, L, 16)))
def setup_inputs_spread(rng):
    a = np.exp2(8 * rng.random((N, 8, 16, I))); b = np.exp2(8 * rng.random((N, 8, 1, I))) * rng.random((N, 8, 16, I))
    even = (rng.permutation(8) < 5)[None, :, None, None]
    F = np.minimum(np.where(even, a, b).astype(np.int64), 255) * (rng.random((N, 8, 1, I)) > 0.0625)
    low = (rng.permutation(8) < 4)[None, :, None]
    v = (I * rng.random((N, 8, I)) ** 3).astype(np.int64); sel = np.where(low, v, I - 1 - v)
    w = (I * rng.random((N, 8, L, 16)) ** 2).astype(np.int64); P = np.where(low[..., None], I - 1 - w, w)
    return pack(F, sel, P)
def setup_inputs_ends(rng):
    hi = rows8(rng); up = np.where(hi, np.add.accumulate(hi.astype(np.int64), axis=2), np.add.accumulate((~hi).astype(np.int64), axis=2)) - 1
    cl = rng.choice(np.array([0, 1, 1, 1, 2, 2, 2]), (N, 8, I))
    cl[..., [0, 1]] = 2; cl[..., I - 1] = 1; cl[..., [2, 3, I - 2]] = 3; cl[..., [4, 5, I - 3]] = 0
    off = rng.integers(0, 8, (2, N, 8, 1, I)); off[..., [0, 1, I - 1]] = 8; c = cl[:, :, None, :]
    F = 255 * ((c == 3) | ((c > 0) & ((c == 1) == hi) & (up != off[0]) & (up != off[1]))).astype(np.int64)
    F[..., 1] = np.where((~hi & (up == 7))[..., 0], 254, F[..., 1]); F[:, :, 15, 3] = 254
    for g in range(8): F[:, g, 2 * g + 1, 5] = 1
    sel = np.where(rng.random((N, 8, I)) < 0.75, (I - 1) * rng.integers(0, 2, (N, 8, I)), rng.integers(0, I, (N, 8, I)))
    cross = rng.random((N, 8)) < 0.3; cross[0, 0] = False; cross[N - 1, 7] = False; cross[0, 7] = True
    sel[..., 0] = np.where(cross, I - 1, 0); sel[..., I - 1] = np.where(cross, 0, I - 1); sel[..., 1] = 1
    inner = of_class(rng, cl, rng.choice(np.array([0, 1, 1, 1, 2, 2, 2]), (N, 8, L, 16)), 4)
    P = np.where(rng.random((N, 8, L, 16)) < 0.75, np.where(rng.random((N, 8, L, 16)) < rng.random((N, 8, L, 1)), I - 1, 0), inner)
    P[:, :, L - 1] = 1; P[:, :, L - 1, 15] = I - 1; P[:, :, 0] = 1; P[:, :, 0, 8] = I - 1
    P[:, :, L - 2] = 3; P[:, :, L - 2, 12:14] = 0
    P[:, ::2, L - 2, 5] = 2; P[:, ::2, L - 2, 10] = I - 2; P[:, 1::2, L - 2, 5] = I - 2; P[:, 1::2, L - 2, 10] = 2; P[:, :, L - 2, 15] = I - 2
    P[:, :, L - 3] = 4; P[:, :, L - 3, ::3] = I - 3
    P[:, :, L - 4] = 4; P[:, :, L - 4, 3] = 5; P[:, :, L - 4, 15] = 5
    P[::2, :, S] = 4; P[::2, :, S, ::3] = I - 3
    P[1::2, :, S] = 3; P[1::2, :, S, 9] = 2; P[1::2, :, S, 12] = I - 2
    return pack(F, sel, P)
def setup_inputs_corners(rng):
    n = T + 3; hi = rows8(rng); cl = np.argsort(rng.random((N, 8, I)), axis=-1) % n
    u = rng.random((N, 8, 16, I)); c = cl[:, :, None, :]; tall = c == T + 2
    F = np.where(c == 0, 8 * u, np.where(tall == hi, np.where(tall, 208 + 48 * u, 128 + 32 * u), np.where(tall, 8 + 33 * u, 41 * u))).astype(np.int64)
    own = np.arange(I)[None, None, :]; z = rng.integers(0, 3, (N, 8, I)); step = of_class(rng, cl, np.maximum(np.minimum(cl, T) - 1, 0), n)
    sel = np.where(cl == T + 1, own, np.where((cl == 0) | (cl == T + 2), np.where(z == 0, own, np.where(z == 1, 0, I - 1)), step))
    fm = rng.integers(0, 12, (N, 8, 1)); fm[0, 0] = 2; fm[N - 1, 7] = 1; fm[0, 7] = 6; fm[N - 1, 0] = 2; fm[1, 3] = 4; fm[2, 5] = 7
    md = np.where(fm < 6, fm, rng.integers(0, 6, (N, 8, L)))[..., None]
    one = np.arange(16) == rng.integers(0, 16, (N, 8, L, 1)); dd = rng.integers(0, T + 1, (N, 8, L, 1)); mix = rng.integers(0, n, (N, 8, L, 16))
    want = np.where(md == 0, mix, np.where(md == 1, T + 2, np.where(md == 2, np.where(one, T + 2, T + 1), np.where(md == 3, np.where(one, mix, T + 2), np.where(md == 4, np.where(one, T + 2, dd), T + 1)))))
    P = of_class(rng, cl, want, n); P = np.where(md == 1, P[..., :1], P)
    P[:, ::2, 1] = 0; P[:, 1::2, L - 1] = I - 1
    return pack(F, sel, P)
def setup_inputs_ties(rng):
    kind = rng.choice(np.array([0, 1, 1, 2, 2, 3, 4]), (N, 8, I)); rk = np.argsort(rng.random((N, 8, 16, I), dtype=np.float32), axis=2)
    more = np.array([0, 16 - H, 17 - H, 3, 0])[kind][:, :, None, :]; less = np.array([16, 16 - H, 17 - H, 13, 8])[kind][:, :, None, :]
    F = rng.integers(100, 200, (1, 8, 16, 1)) + (rk < more).astype(np.int64) - (rk >= less).astype(np.int64)
    two = rng.permutation(8)[:2]; x = int(rng.integers(0, N))
    for r in (x, (x - 1) % N):
        F[r, two[0]] += 20; F[r, two[1]] += 20
        v = rng.permutation(I)[:I // 16]; F[r, two[1], rng.integers(0, 16, v.size), v] = 0
    return pack(F, rng.integers(0, I, (N, 8, I)), rng.integers(0, I, (N, 8, L, 16)))
def check_inputs(d):
    bad = []
    for k, hi in (("front", 255), ("sel0", I - 1), ("par", I - 1)):
        x = np.asarray(d[k]).astype(np.float64)
        if not (np.min(x) >= 0 and np.max(x) <= hi): bad.append("range of " + k)
        elif np.any(x != np.floor(x)): bad.append("whole numbers in " + k)
    return bad
def reference(front, sel0, par):
    F = np.zeros((N, 8, 16, W), np.int32); F[..., :I] = front.astype(np.float32).reshape(N, 8, 16, I).astype(np.int32)
    sel = np.zeros((N, 8, W), np.int64); sel[..., :I] = sel0
    P = np.stack([gentries(a) for a in par]).astype(np.int64).reshape(N, 8, L, 16)
    i = np.arange(L); k = np.arange(16)
    def fronts(q):
        return np.take_along_axis(F, q.reshape(N, 8, 1, L * 16), 3).reshape(N, 8, 16, L, 16)
    for t in range(R):
        b = I + t * (L + M)
        f = fronts(P); s = np.argmax(np.add.reduce(f, axis=2), axis=3)
        ps = np.take_along_axis(P, s[..., None], 3)[..., 0]; g = np.take_along_axis(F, ps[:, :, None, :], 3)
        q = P; c = np.zeros(P.shape, np.int64); walk = np.ones(P.shape, bool)
        for test in range(T):
            fq = f if test == 0 else fronts(q)
            walk = walk & (np.add.reduce((fq <= g[..., None]).astype(np.int32), axis=2) < H)
            c = c + walk.astype(np.int64)
            q = np.where(walk, np.take_along_axis(sel, q.reshape(N, 8, L * 16), 2).reshape(q.shape), q)
        red = c == T
        new = np.maximum.reduce(fronts(np.where(red, ps[..., None], q)), axis=4)
        new[:, :, (i + t) & 15, i] = np.minimum(255, new[:, :, (i + t) & 15, i] + 1)
        come = np.roll(new[..., ::S], 1 + t % (N - 1), axis=0)
        best = np.argmax(np.add.reduce((f[:, :, :, ::S] <= come[..., None]).astype(np.int32), axis=2), axis=3)
        F[..., b:b + L] = new; F[..., b + L:b + L + M] = come
        sel[..., b:b + L] = ps; sel[..., b + L:b + L + M] = np.take_along_axis(P[:, :, ::S], best[..., None], 3)[..., 0]
        sc = np.add.reduce(c, axis=3)[..., None]; reds = np.add.reduce(red.astype(np.int64), axis=(1, 3))[:, None, :, None]
        P = np.where(k == s[..., None], b + i[:, None], np.where(red, b + ((5 * i[:, None] + 37 * k + sc + reds) & (L - 1)), np.where(c == 0, b + L + ((i[:, None] + k + reds) & (M - 1)), q)))
    return {"yf": np.ascontiguousarray(F[..., I:]).reshape(N, 128, W - I).astype(np.float32).astype(BF), "ys": np.ascontiguousarray(sel[..., I:]).astype(np.float32),
            "yp": np.ascontiguousarray(P.transpose(0, 1, 3, 2)).reshape(N, 128, L).astype(np.float32)}

from concourse.mybir import dt, AluOpType, AxisListType, ActivationFunctionType

OP = AluOpType
AF = ActivationFunctionType
W = 3520
I0, RN = 2560, 320
SIG = (0, 2, 1, 3)
NENG = 4
FA = 80
TS = 64
FB = 72

_s = "sbuf"
_b, _f, _i, _u = "bfloat16", "float32", "int32", "uint16"
SCRATCH = {
    "FX": (_s, [128, 4 * W], _b), "NX": (_s, [128, 4 * W], _b), "OWN": (_s, [128, W], _b),
    "PI": (_s, [128, 256], _i), "YI": (_s, [80, 256], _i), "YF": (_s, [80, 256], _f), "XI": (_s, [128, 160], _i),
    "XH": (_s, [128, 160], _i), "XL": (_s, [128, 160], _i), "XHB": (_s, [128, 160], _b), "XLB": (_s, [128, 160], _b),
    "SL": (_s, [128, 160], _u), "OH": (_s, [8, W], _b), "OL": (_s, [8, W], _b),
    "F00": (_s, [128, 4096], _b), "F01": (_s, [128, 4096], _b),
    "L0": (_s, [128, 4096], _b), "L1": (_s, [128, 4096], _b), "L2": (_s, [128, 4096], _b),
    "GS": (_s, [128, 4096], _b), "GE": (_s, [128, 4096], _b),
    "FQ": (_s, [128, 4096], _b), "MX": (_s, [128, 4096], _b), "NG": (_s, [128, 4096], _b),
    "RS": (_s, [128, 1024], _b), "RE": (_s, [128, 1024], _b), "LR": (_s, [128, 1024], _b),
    "P32a": (_s, [128, 256], _f), "P32b": (_s, [128, 256], _f), "PUa": (_s, [128, 256], _u), "PUb": (_s, [128, 256], _u),
    "LU": (_s, [128, 256], _u), "KM": (_s, [128, 384], _f), "LI": (_s, [128, 24], _i), "LO": (_s, [128, 24], _i),
    "YW": (_s, [128, 3 * 160], _b), "OF": (_s, [128, 32], _u),
    "E0": (_s, [128, 256], _b), "E1": (_s, [128, 256], _b), "E2": (_s, [128, 256], _b),
    "MS": (_s, [128, 320], _b), "M0": (_s, [128, 256], _b), "PR": (_s, [128, 320], _f),
    "W1": (_s, [128, 256], _b), "W2": (_s, [128, 256], _b), "W3": (_s, [128, 256], _b),
    "X1": (_s, [128, 256], _i), "X2": (_s, [128, 256], _i), "Z1": (_s, [128, 256], _i), "Z2": (_s, [128, 256], _i),
    "DMK": (_s, [128, 320], _f), "DSC": (_s, [128, 320], _f), "PL": (_s, [128, 20], _u),
    "SM": (_s, [128, 256], _b), "NB0": (_s, [128, 256], _b), "NB1": (_s, [128, 256], _b), "NB2": (_s, [128, 256], _b),
    "RB0": (_s, [128, 64], _b), "RB1": (_s, [128, 64], _b), "RB2": (_s, [128, 64], _b),
    "RL0": (_s, [128, 64], _b), "RL1": (_s, [128, 64], _b), "RL2": (_s, [128, 64], _b),
    "YSB": (_s, [128, 960], _f), "YPB": (_s, [128, 256], _f),
    "ON": (_s, [128, 128], _b), "ID": (_s, [128, 128], _b), "NI": (_s, [128, 128], _b), "I32": (_s, [128, 128], _f),
    "BO": (_s, [128, 128], _b), "BT": (_s, [128, 128], _b), "B32": (_s, [128, 128], _f), "G8": (_s, [128, 8], _b), "G8T": (_s, [128, 8], _b), "S8": (_s, [128, 8], _b),
    "ZA": (_s, [128, 144], _b), "ZN": (_s, [128, 144], _b), "ZH": (_s, [128, 144], _b), "CC": (_s, [128, 128], _b),
    "WI": (_s, [128, 128], _b), "BI": (_s, [128, 128], _b), "CI": (_s, [128, 128], _b),
    "MK": (_s, [128, 2048], _b), "D0": (_s, [128, 128], _f), "KA": (_s, [128, 8], _b), "KB": (_s, [128, 8], _b),
    "PX": (_s, [128, 8], _i), "PK": (_s, [128, 8], _i), "KC": (_s, [128, 8], _f), "HF": (_s, [128, 8], _f),
    "IZ": (_s, [128, 256], _i), "IA": (_s, [128, 256], _i), "IC": (_s, [128, 256], _b),
    "CT1": (_s, [128, 256], _f), "CT2": (_s, [128, 256], _f),
    "IN0": (_s, [128, 256], _b), "IN1": (_s, [128, 256], _b), "IN2": (_s, [128, 256], _b),
    "DZ": (_s, [128, 320], _i), "DY": (_s, [128, 320], _i), "DM": (_s, [128, 320], _b),
    "q0": ("psum", [128, 512], _f), "q1": ("psum", [128, 512], _f), "q2": ("psum", [128, 512], _f), "q3": ("psum", [128, 512], _f),
    "q4": ("psum", [128, 512], _f), "q5": ("psum", [128, 512], _f), "q6": ("psum", [128, 512], _f), "q7": ("psum", [128, 512], _f),
}
SEMAPHORES = ["qv", "qs", "qt", "qg"] + ["d%d" % k for k in range(24)] + ["rc0", "rc1", "rc2", "rl0", "rl1", "rl2", "lo0", "lo1", "lo2"]


def route(core, t, T, topo):
    n = len(T.cores)
    dst = T.cores[(T.cores.index(core) + 1 + t % 7) % n]
    if topo.may_write(core, dst):
        return dst, None
    via = [c for c in topo.cores_of(core) if c != core and topo.may_write(core, c) and topo.may_write(c, dst) and c not in T.cores]
    via.sort(key=lambda c: (topo.die(c) != topo.die(core), c))
    return dst, via[0]


def send(g, T, topo, src, dst, out, inp, rsem, lsem):
    rid, pid = topo.addr(dst, src)
    m = 0
    for e in topo.engines(src, dst)[:NENG]:
        m |= 1 << e
    return g.remote_dma(out, inp, rsem, lsem, pid, rid, m)


def helper(g, core, T, topo):
    for t in range(3):
        for r in T.cores:
            dst, via = route(r, t, T, topo)
            if via == core:
                g.wait_ge(T.sem["rl%d" % t], NENG)
                send(g, T, topo, core, dst, T["RB%d" % t][:], T["RL%d" % t][:], T.sem["rc%d" % t], T.sem["lo%d" % t])
                g.wait_ge(T.sem["lo%d" % t], NENG)


def rank_program(g, core, T, topo):
    if T.rank_of(core) is None:
        helper(g, core, T, topo)
        return
    eng = {"v": g.vector, "s": g.scalar, "t": g.tensor, "y": g.sync, "g": g}
    cnt = {"v": 0, "s": 0, "t": 0, "g": 0}
    tot = {}
    known = {q: {} for q in eng}
    acc = {}

    def R(name, lo=0, hi=None, st=1, p1=128, p0=0, pst=1):
        if hi is None:
            hi = SCRATCH[name][1][1]
        return (name, lo, hi, st, p0, p1, pst, None)

    def IX(win, off):
        return win[:7] + (off,)

    def A(x):
        name, lo, hi, st, p0, p1, pst, off = x
        ps = slice(p0, p1) if pst == 1 else slice(p0, p1, pst)
        r = T[name][ps, lo:hi] if st == 1 else T[name][ps, lo:hi:st]
        return r if off is None else r.indirect(A(off))

    def overlap(a, b):
        if a[2] <= b[1] or b[2] <= a[1] or a[5] <= b[4] or b[5] <= a[4]:
            return False
        if a[3] == b[3] and a[3] > 1 and (a[1] - b[1]) % a[3]:
            return False
        if a[6] > 1 and a[6] == b[6] and (a[4] - b[4]) % a[6]:
            return False
        return True

    def waits(q, reads, writes):
        need = []
        for x, wr in [(r, False) for r in reads] + [(w, True) for w in writes]:
            ps = SCRATCH[x[0]][0] == "psum"
            for (y, ywr, yq, tok, snap) in acc.get(x[0], ()):
                if ps and yq != q:
                    need.append((tok, snap))
                elif (wr or ywr) and overlap(x, y):
                    if yq == q == "t":
                        continue
                    need.append((tok, snap))
        best = {}
        for (sem, val), snap in need:
            v = tot[sem] if val is None else val
            if sem not in best or v > best[sem][0]:
                best[sem] = (v, snap)
        k = known[q]
        for sem in sorted(best, key=lambda s: -sum(best[s][1].values())):
            v, snap = best[sem]
            if k.get(sem, 0) >= v:
                continue
            k[sem] = v
            for a, b in snap.items():
                k[a] = max(k.get(a, 0), b)
            eng[q].wait_ge(T.sem[sem], v)

    def note(q, reads, writes, tok):
        snap = dict(known[q])
        for x in writes:
            L = acc.setdefault(x[0], [])
            L[:] = [e for e in L if not (x[1] <= e[0][1] and x[2] >= e[0][2] and x[3] == 1 and x[4] <= e[0][4] and x[5] >= e[0][5] and x[6] == 1)]
            L.append((x, True, q, tok, snap))
        for x in reads:
            L = acc.setdefault(x[0], [])
            L[:] = [e for e in L if not (e[0] == x and e[2] == q and not e[1] and tok[1] is not None and e[3][1] is not None)]
            L.append((x, False, q, tok, snap))

    def ex(xs):
        r = []
        for x in xs:
            if isinstance(x, tuple):
                r.append(x[:7] + (None,))
                if x[7] is not None:
                    r.append(x[7])
        return r

    def emit(q, call, out, ins):
        rd, wr = ex(ins), ex([out])
        waits(q, rd, wr)
        cnt[q] += 1
        call().then_inc(T.sem["q" + q], 1)
        note(q, rd, wr, ("q" + q, cnt[q]))

    def S(x):
        return A(x) if isinstance(x, tuple) else x

    def vcopy(out, i):
        emit("v", lambda: g.vector.tensor_copy(A(out), A(i)), out, [i])

    def vtt(out, a, b, op):
        emit("v", lambda: g.vector.tensor_tensor(A(out), A(a), A(b), op), out, [a, b])

    def vts(out, a, s1, op0, s2=None, op1=None):
        if op1 is None:
            emit("v", lambda: g.vector.tensor_scalar(A(out), A(a), S(s1), None, op0), out, [a, s1])
        else:
            emit("v", lambda: g.vector.tensor_scalar(A(out), A(a), S(s1), S(s2), op0, op1), out, [a, s1, s2])

    def vscan(out, a, b, op0, op1):
        emit("v", lambda: g.vector.tensor_tensor_scan(A(out), A(a), A(b), 0.0, op0, op1), out, [a, b])

    def vset(out, c):
        emit("v", lambda: g.vector.memset(A(out), c), out, [])

    def act(out, i, fn=AF.Copy, bias=None, scale=1.0):
        if bias is None:
            emit("s", lambda: g.scalar.activation(A(out), A(i), fn, scale=scale), out, [i])
        else:
            emit("s", lambda: g.scalar.activation(A(out), A(i), fn, bias=A(bias), scale=scale), out, [i, bias])

    def mm(out, l, r, start, stop):
        emit("t", lambda: g.tensor.matmul(A(out), A(l), A(r), start, stop), out, [l, r])

    def copy(q, out, i):
        if q == "s":
            act(out, i)
        else:
            vcopy(out, i)

    def gather(q, out, win, off):
        copy(q, out, IX(win, off))

    def dma(q, sem, out, i):
        rd = ex([i]) if isinstance(i, tuple) else []
        wr = ex([out]) if isinstance(out, tuple) else []
        waits(q, rd, wr)
        eng[q].dma_start(S(out), S(i)).then_inc(T.sem[sem], 16)
        tot[sem] = tot.get(sem, 0) + 16
        note(q, rd, wr, (sem, None))

    def sel(out, i, pat, op, base, cm):
        emit("g", lambda: g.affine_select(A(out), A(i), pat, op, 0.0, base, cm), out, [i])

    def iota(out, pat, base, cm, flag=False):
        emit("g", lambda: g.iota(A(out), pat, base, cm, allow_small_or_imprecise_dtypes=flag) if flag else g.iota(A(out), pat, base, cm), out, [])

    dma("y", "d0", R("PI"), T.par[:])
    dma("y", "d1", R("FX", 0, I0), T.front[:])
    for h in range(2):
        for k in range(8):
            dma("s" if h else "y", "d2" if h else "d3", R("YI", 128 * h + 16 * k, 128 * h + 16 * k + 16, p1=80), T.sel0[k, 1280 * h:1280 * h + 1280])
    dma("y", "d4", R("XI"), T.sel0[:])

    iota(R("PX"), [[0, 8]], 0, 1)
    vset(R("ON"), 1.0)
    vset(R("MK"), 1.0)
    vset(R("MK", 0, 2048, 16), 0.0)
    vset(R("ZA"), 0.0)
    vset(R("ZN"), 0.0)
    vset(R("ZH"), 0.0)
    vset(R("CC"), 0.04)
    vset(R("YW"), 0.0)
    vset(R("D0"), 1.0)
    vset(R("D0", 0, 128, 16), -3e7)
    vset(R("HF"), 0.5)
    vset(R("GS"), 0.0)
    sel(R("G8T"), R("ON", 0, 8), [[-16, 8]], OP.is_ge, 0, 1)
    sel(R("G8"), R("G8T"), [[16, 8]], OP.is_ge, 15, -1)
    sel(R("ID"), R("ON"), [[-1, 128]], OP.is_equal, 0, 1)
    sel(R("BT"), R("ON"), [[-16, 8], [0, 16]], OP.is_ge, 0, 1)
    sel(R("BO"), R("BT"), [[16, 8], [0, 16]], OP.is_ge, 15, -1)
    iota(R("KA"), [[256, 8]], 0, 0, True)
    iota(R("NX", 0, W), [[0, W]], 0, 0, True)
    iota(R("IC"), [[1, 2], [2, 2], [4, 64]], 0, 0, True)
    iota(R("IZ"), [[1, 2], [2, 2], [4, 64]], 0, -1)
    iota(R("DZ"), [[1, 320]], 0, -1)
    iota(R("OH", p1=8), [[64, 55], [0, 64]], 0, 0, True)
    iota(R("OL", p1=8), [[0, 55], [1, 64]], 0, 0, True)
    for m in range(4):
        vcopy(R("PUa", 64 * m, 64 * m + 64), R("PI", SIG[m], 256, 4))
    vts(R("PK"), R("PX"), 15, OP.bitwise_and)
    vts(R("KC", 0, 1), R("PK", 0, 1), -1.0, OP.mult, 15.0, OP.add)
    vts(R("KC", 1, 2), R("PK", 0, 1), 37.0, OP.mult)
    vts(R("KC", 2, 3), R("PK", 0, 1), 1.0, OP.mult)
    vts(R("KB"), R("PK"), 16.0, OP.mult, 15.0, OP.add)
    vts(R("S8"), R("G8"), 16.0, OP.mult)
    vts(R("ZA", 15, 143, 16), R("G8"), 0.08, OP.mult)
    vts(R("ZH", 15, 143, 16), R("G8"), 0.04, OP.mult)
    vts(R("KC", 3, 4), R("KC", 2, 3), 2.0, OP.is_lt)
    vts(R("ZN", 15, 143, 16), R("G8"), R("KC", 3, 4), OP.mult)
    act(R("NI"), R("ID"), scale=-1.0)
    act(R("I32"), R("ID"))
    act(R("B32"), R("BO"))
    act(R("WI"), R("ID"), scale=float(W))
    vcopy(R("YF", p1=80), R("YI", p1=80))
    for h in range(2):
        mm(R("q7", 80 * h, 80 * h + 80), R("YF", 128 * h, 128 * h + 128, p1=80), R("I32", 0, 80, p1=80), True, True)
    vcopy(R("SL"), R("q7", 0, 160))

    def own1():
        for m in range(4):
            vcopy(R("P32a", 64 * m, 64 * m + 64), R("PI", SIG[m], 256, 4))
        vset(R("RS"), 0.0)
        vts(R("XH"), R("XI"), 4032, OP.bitwise_and)
        vts(R("XL"), R("XI"), 63, OP.bitwise_and)
        vcopy(R("XHB"), R("XH"))
        vcopy(R("XLB"), R("XL"))

    def own2():
        dma("y", "d5", R("NX", 3 * W, 4 * W), R("NX", 0, W))
        dma("y", "d6", R("FX", 3 * W, 4 * W), R("NX", 0, W))
        dma("y", "d7", R("NX", W, W + I0), R("NX", 0, I0))
        dma("y", "d8", R("OWN"), R("NX", 0, W))
        for l in range(3):
            dma("y", "d18", R("FX", l * W + I0, l * W + W), R("NX", 0, W - I0))
        for l in range(1, 3):
            dma("y", "d19", R("NX", l * W + I0, l * W + W), R("NX", 0, W - I0))
        dma("y", "d9", R("NX", W, W + I0, p0=0, p1=128, pst=16), R("XHB"))
        dma("y", "d10", R("NX", W, W + I0, p0=1, p1=128, pst=16), R("XLB"))
        dma("y", "d11", R("OWN", p0=0, p1=128, pst=16), R("OH", p1=8))
        dma("y", "d12", R("OWN", p0=1, p1=128, pst=16), R("OL", p1=8))

    def consts2():
        vts(R("IA"), R("IZ"), 15, OP.bitwise_and)
        for t in range(3):
            vts(R("IN%d" % t), R("IA"), float((16 - t) % 16), OP.is_equal)
        vts(R("DY"), R("DZ"), 15, OP.bitwise_and)
        vts(R("DM"), R("DY"), 0.0, OP.is_equal)

    def f0(t):
        return "F0%d" % (t % 2)

    def pu(t):
        return "PUa" if t % 2 == 0 else "PUb"

    def p32(t):
        return "P32a" if t % 2 == 0 else "P32b"

    def first(t, X, q, l0, l1):
        c = 128 * X
        gather(q, R(f0(t), 2048 * X + 16 * l0, 2048 * X + 16 * l1), R("FX", 0, I0 + RN * t), R(pu(t), c + l0, c + l1))

    def argmax_p(src, base, n, z):
        for k in range(16):
            mm(R("q2", 128 * z + k, 128 * z + 128, 16, p1=n), R(src, base + k, base + 16 * n, 16), R("S8"), True, True)

    def argmax_v(n, z):
        vscan(R("KM", 128 * z, 128 * z + 128, p1=n), R("D0", p1=n), R("q2", 128 * z, 128 * z + 128, p1=n), OP.add, OP.max)
        vcopy(R("LI", 8 * z, 8 * z + 8, p1=n), R("KM", 128 * z + 15, 128 * z + 128, 16, p1=n))
        vts(R("LO", 8 * z, 8 * z + 8, p1=n), R("LI", 8 * z, 8 * z + 8, p1=n), 15, OP.bitwise_and)
        vcopy(R("YW", 160 * z + 15, 160 * z + 143, 16, p1=n), R("LO", 8 * z, 8 * z + 8, p1=n))

    def choice1p(t, X):
        argmax_p(f0(t), 2048 * X, 128, X)

    def choice1v(X):
        argmax_v(128, X)

    def choice2p(X):
        o = R("q6", 8 * X, 8 * X + 8)
        mm(o, R("ID"), R("KA"), True, False)
        mm(o, R("ID"), R("KB"), False, False)
        for w in range(16):
            mm(o, R("YW", 160 * X + 15 - w, 160 * X + 143 - w), R("NI", w, 128, 16), False, w == 15)

    def choice2v(t, X):
        c = 2048 * X
        vcopy(R("OF", 8 * X, 8 * X + 8), R("q6", 8 * X, 8 * X + 8))
        gather("v", R("GS", c, c + 2048, 16), R(f0(t), c, c + 2048), R("OF", 8 * X, 8 * X + 8))
        vscan(R("GE", c, c + 2048), R("MK"), R("GS", c, c + 2048), OP.mult, OP.add)

    def smask_p(X):
        for w in range(16):
            mm(R("q7", 128 * X, 128 * X + 128), R("YW", 160 * X + 15 - w, 160 * X + 143 - w), R("ID"), w == 0, w == 15)

    def smask_v(X):
        vts(R("MS", 128 * X, 128 * X + 128), R("q7", 128 * X, 128 * X + 128), R("KC", 0, 1), OP.is_equal)

    def sign(c, src, res, b):
        mm(R(b), R("ID"), R("GE", c, c + 512), True, False)
        mm(R(b), R("NI"), R(src, c, c + 512), False, True)
        act(R(res, c, c + 512), R(b), AF.Sign, R("HF", 0, 1))

    def test0(t, X, n):
        sign(2048 * X + 512 * n, f0(t), "L0", "q%d" % (n % 2))

    def raw(t, X, d, l0, l1):
        c = 2048 * X
        gather("s", R("FQ", c + 16 * l0, c + 16 * l1), R("FX", d * W, d * W + I0 + RN * t), R(pu(t), 128 * X + l0, 128 * X + l1))

    def rawtest(X, d, l0, l1):
        for c in range(2048 * X + 16 * l0, 2048 * X + 16 * l1, 512):
            sign(c, "FQ", "L%d" % d, "q%d" % (c // 512 % 2))

    def test(t, X, d, l0=0, l1=128):
        c = 2048 * X
        vtt(R("L%d" % d, c + 16 * l0, c + 16 * l1), IX(R("FX", d * W, d * W + I0 + RN * t), R(pu(t), 128 * X + l0, 128 * X + l1)), R("GE", c + 16 * l0, c + 16 * l1), OP.is_le)

    def count(X, d, l0=0, l1=128, signs=False):
        c = 2048 * X
        o = R("q%d" % (3 + d), l0, l1)
        if signs:
            mm(o, R("BO"), R("CC", 0, l1 - l0), True, False)
        for k in range(16):
            mm(o, R("ZH" if signs else "ZA", 15 - k, 143 - k), R("L%d" % d, c + 16 * l0 + k, c + 16 * l1, 16), k == 0 and not signs, k == 15)

    def walked(X, d):
        o, q = R("E%d" % d, 128 * X, 128 * X + 128), R("q%d" % (3 + d), 0, 128)
        if d == 0:
            vts(o, q, 1.0, OP.is_lt)
        else:
            vtt(o, q, R("E%d" % (d - 1), 128 * X, 128 * X + 128), OP.is_lt)

    def list_q(t, X):
        c = 128 * X
        o = R("q6", 128 + c, 256 + c)
        mm(o, R("I32"), R(p32(t), c, c + 128), True, False)
        for d in range(2):
            mm(o, R("WI"), R("E%d" % d, c, c + 128), False, False)

    def list_p(X):
        c = 128 * X
        mm(R("q6", 128 + c, 256 + c), R("WI"), R("E2", c, c + 128), False, True)

    def list_v(X):
        vcopy(R("LU", 128 * X, 128 * X + 128), R("q6", 128 + 128 * X, 256 + 128 * X))

    def entered(t, X, q, l0, l1):
        c = 2048 * X
        gather(q, R("FQ", c + 16 * l0, c + 16 * l1), R("FX", 0, 3 * W + I0 + RN * t), R("LU", 128 * X + l0, 128 * X + l1))

    def numbers(t, X, q):
        c = 2048 * X
        gather(q, R("NG", c, c + 2048), R("NX", 0, 3 * W + I0 + RN * t), R("LU", 128 * X, 128 * X + 128))

    def newblocks(t, X):
        c = 128 * X
        a, b = 16 * c, 16 * c + 2048
        vscan(R("MX", a, b), R("MK"), R("FQ", a, b), OP.mult, OP.max)
        vtt(R("SM", c, c + 128), R("MX", a + 15, b, 16), R("IN%d" % t, c, c + 128), OP.add)
        vts(R("NB%d" % t, c, c + 128), R("SM", c, c + 128), 255.0, OP.min)

    def publish(t, X, q):
        b = I0 + RN * t
        for m in (2 * X, 2 * X + 1):
            copy(q, R("FX", b + SIG[m], b + 256, 4), R("NB%d" % t, 64 * m, 64 * m + 64))

    def publish1(t, X, q):
        b = W + I0 + RN * t
        for m in (2 * X, 2 * X + 1):
            copy(q, R("FX", b + SIG[m], b + 256, 4), R("GS", 1024 * m, 1024 * m + 1024, 16))

    def away(t):
        dst, via = route(core, t, T, topo)
        nb = R("NB%d" % t, 0, 64)
        waits("g", [nb], [])
        lo = "lo%d" % t
        if via is None:
            send(g, T, topo, core, dst, T["RB%d" % t][:], A(nb), T.sem["rc%d" % t], T.sem[lo])
        else:
            send(g, T, topo, core, via, T["RL%d" % t][:], A(nb), T.sem["rl%d" % t], T.sem[lo])
        tot[lo] = NENG
        note("g", [nb], [], (lo, NENG))

    def landed(t, q):
        b = I0 + RN * t + 256
        copy(q, R("FX", b, b + 64), R("RB%d" % t))

    def rename_p(X):
        c = 128 * X
        ca, ab = R("q7", 256, 384), R("q7", 384, 512)
        for d in range(3):
            mm(ca, R("BO"), R("E%d" % d, c, c + 128), d == 0, False)
        mm(ca, R("ON"), R("E2", c, c + 128), False, True)
        mm(ab, R("ON"), R("E2", c, c + 128), True, True)

    def rename_v(X):
        c = 128 * X
        vtt(R("X1", c, c + 128), R("q7", 256, 384), R("CT1", c, c + 128), OP.add)
        vtt(R("X2", c, c + 128), R("q7", 384, 512), R("CT2", c, c + 128), OP.add)
        vts(R("Z1", c, c + 128), R("X1", c, c + 128), 255, OP.bitwise_and)
        vts(R("Z2", c, c + 128), R("X2", c, c + 128), 63, OP.bitwise_and)
        vtt(R("M0", c, c + 128), R("MS", c, c + 128), R("E0", c, c + 128), OP.is_equal)
        vtt(R("W3", c, c + 128), R("MS", c, c + 128), R("IC", c, c + 128), OP.mult)
        vtt(R("W1", c, c + 128), R("E2", c, c + 128), R("Z1", c, c + 128), OP.mult)
        vtt(R("W2", c, c + 128), R("M0", c, c + 128), R("Z2", c, c + 128), OP.mult)

    def renamed_p(X):
        c = 128 * X
        o = R("q3", 128, 256)
        mm(o, R("BI"), R("MS", c, c + 128), True, False)
        mm(o, R("BI"), R("E2", c, c + 128), False, False)
        mm(o, R("CI"), R("M0", c, c + 128), False, False)
        for k in range(3):
            mm(o, R("ID"), R("W%d" % (k + 1), c, c + 128), False, False)
        for k in range(16):
            mm(o, R("ZN", 15 - k, 143 - k), R("NG", 16 * c + k, 16 * c + 2048, 16), False, k == 15)

    def renamed_v(t, X):
        c = 128 * X
        if t < 2:
            vcopy(R(pu(t + 1), c, c + 128), R("q3", 128, 256))
        else:
            for h in range(2):
                vcopy(R("YPB", SIG[2 * X + h], 256, 4), R("q3", 128 + 64 * h, 192 + 64 * h))

    def renamed_s(t, X):
        if t < 2:
            act(R(p32(t + 1), 128 * X, 128 * X + 128), R("q3", 128, 256))

    def base(t):
        act(R("BI"), R("ID"), scale=float(I0 + RN * t))
        act(R("CI"), R("ID"), scale=float(I0 + RN * t + 256))

    def chosen_v(t, X):
        c = 128 * X
        vtt(R("PR", c, c + 128), R("MS", c, c + 128), R(p32(t), c, c + 128), OP.mult)

    def chosen_p(X):
        for m in (2 * X, 2 * X + 1):
            mm(R("q5", 128 + SIG[m], 384, 4), R("B32"), R("PR", 64 * m, 64 * m + 64), True, True)

    def received1(t):
        act(R("RS", 0, 1024, 16), R("RB%d" % t))
        vscan(R("RE"), R("MK", 0, 1024), R("RS"), OP.mult, OP.add)

    def received1p(t):
        for n in range(2):
            d = "q%d" % n
            mm(R(d), R("ID"), R("RE", 512 * n, 512 * n + 512), True, False)
            mm(R(d), R("NI"), R(f0(t), 512 * n, 512 * n + 512), False, True)
            act(R("LR", 512 * n, 512 * n + 512), R(d), AF.Sign, R("HF", 0, 1))

    def received2p():
        argmax_p("LR", 0, 64, 2)

    def received2v():
        argmax_v(64, 2)

    def received3p():
        for w in range(16):
            mm(R("q5", 448, 512), R("YW", 320 + 15 - w, 320 + 143 - w, p1=64), R("ID", 0, 64, p1=64), w == 0, w == 15)

    def received3v(t):
        vts(R("MS", 256, 320), R("q5", 448, 512), R("KC", 0, 1), OP.is_equal)
        vtt(R("PR", 256, 320), R("MS", 256, 320), R(p32(t), 0, 64), OP.mult)

    def received4p():
        mm(R("q5", 384, 448), R("B32"), R("PR", 256, 320), True, True)

    def selected(t):
        act(R("YSB", RN * t, RN * t + RN), R("q5", 128, 448))

    def parents(t, c0, c1):
        vtt(R("DMK", c0, c1), R("q5", 128 + c0, 128 + c1), R("DM", c0, c1), OP.mult)
        vscan(R("DSC", c0, c1), R("MK", c0, c1), R("DMK", c0, c1), OP.mult, OP.add)
        vcopy(R("PL", c0 // 16, c1 // 16), R("DSC", c0 + 15, c1, 16))

    def tables(t, c0, c1, q, what):
        b = I0 + RN * t
        L = R("PL", c0 // 16, c1 // 16)
        if what == "1":
            gather(q, R("FX", W + b + c0, W + b + c1), R("FX", 0, b), L)
        if what == "2":
            gather(q, R("FX", 2 * W + b + c0, 2 * W + b + c1), R("FX", W, W + b), L)
        if what == "n":
            gather(q, R("NX", W + b + c0, W + b + c1), R("OWN", 0, b), L)
            gather(q, R("NX", 2 * W + b + c0, 2 * W + b + c1), R("NX", W, W + b), L)

    for t in range(3):
        acc["RB%d" % t] = [(R("RB%d" % t), True, "x", ("rc%d" % t, NENG), {})]
    for t in range(3):
        if t == 0:
            first(0, 0, "s", 0, 128)
            gather("v", R("FX", W, W + I0), R("FX", 0, I0), R("SL"))
            first(0, 1, "s", 0, 128)
            choice1p(0, 0)
            choice1v(0)
            choice2p(0)
            choice1p(0, 1)
            choice2v(0, 0)
            gather("s", R("FX", 2 * W, 2 * W + I0), R("FX", W, W + I0), R("SL"))
            act(R("CT1"), R("IC"), AF.Identity, R("KC", 1, 2), 5.0)
            act(R("CT2"), R("IC"), AF.Identity, R("KC", 2, 3))
            for n in range(4):
                test0(t, 0, n)
            own1()
            own2()
            test(t, 0, 1, 0, 64)
            test(t, 0, 1, 64, 128)
            gather("s", R("NX", 2 * W, 2 * W + I0), R("NX", W, W + I0), R("SL"))
        else:
            received2p()
            rename_p(1)
            first(t, 0, "s", 0, FA)
            first(t, 0, "v", FA, 128)
            received2v()
            numbers(t - 1, 1, "s")
            received3p()
            choice1p(t, 0)
            rename_v(1)
            received3v(t - 1)
            received4p()
            choice1v(0)
            choice2p(0)
            parents(t - 1, 256, 320)
            renamed_p(1)
            choice2v(t, 0)
            selected(t - 1)
            tables(t - 1, 256, 320, "s", "1")
            renamed_v(t - 1, 1)
            first(t, 1, "s", 0, 64)
            renamed_s(t - 1, 1)
            test(t, 0, 1, 0, 64)
            for n in range(2):
                test0(t, 0, n)
            parents(t - 1, 0, 256)
            tables(t - 1, 0, 320, "s", "2")
            first(t, 1, "s", 64, 128)
            for n in range(2, 4):
                test0(t, 0, n)
            test(t, 0, 1, 64, 128)
            choice1p(t, 1)
        base(t)
        raw(t, 1, 1, 0, TS)
        if t > 0:
            tables(t - 1, 0, 320, "s", "n")
        count(0, 1)
        test(t, 0, 2, 0, 64)
        choice1v(1)
        choice2p(1)
        count(0, 0, signs=True)
        count(0, 2, 0, 64)
        test(t, 0, 2, 64, 128)
        count(0, 2, 64, 128)
        choice2v(t, 1)
        walked(0, 0)
        walked(0, 1)
        list_q(t, 0)
        walked(0, 2)
        list_p(0)
        list_v(0)
        entered(t, 0, "s", 0, 128)
        smask_p(0)
        smask_p(1)
        rename_p(0)
        if t == 0:
            consts2()
        test(t, 1, 1, TS, 128)
        test(t, 1, 2, 0, 64)
        newblocks(t, 0)
        away(t)
        rawtest(1, 1, 0, TS)
        test0(t, 1, 0)
        test0(t, 1, 1)
        count(1, 1, TS, 128)
        test0(t, 1, 2)
        count(1, 1, 0, TS, signs=True)
        test0(t, 1, 3)
        numbers(t, 0, "s")
        count(1, 2, 0, 64)
        count(1, 0, 0, 64, signs=True)
        count(1, 0, 64, 128, signs=True)
        smask_v(0)
        smask_v(1)
        rename_v(0)
        chosen_v(t, 0)
        chosen_v(t, 1)
        test(t, 1, 2, 64, 128)
        count(1, 2, 64, 128)
        walked(1, 0)
        walked(1, 1)
        list_q(t, 1)
        walked(1, 2)
        list_p(1)
        list_v(1)
        received1(t)
        entered(t, 1, "s", 0, FB)
        entered(t, 1, "v", FB, 128)
        received1p(t)
        renamed_p(0)
        chosen_p(0)
        chosen_p(1)
        newblocks(t, 1)
        publish(t, 1, "v")
        renamed_v(t, 0)
        publish(t, 0, "s")
        landed(t, "s")
        if t < 2:
            publish1(t, 0, "s")
            publish1(t, 1, "s")
            renamed_s(t, 0)
    numbers(2, 1, "s")
    rename_p(1)
    rename_v(1)
    received2p()
    received2v()
    received3p()
    received3v(2)
    received4p()
    selected(2)
    renamed_p(1)
    renamed_v(2, 1)
    dma("y", "d14", T.yf[:], R("FX", I0, W))
    dma("y", "d15", T.ys[:], R("YSB", p0=0, p1=128, pst=16))
    dma("y", "d13", T.yp[:], R("YPB"))
    for q in ("v", "s", "t", "g"):
        g.wait_ge(T.sem["q" + q], cnt[q])
    for sem in sorted(tot):
        g.wait_ge(T.sem[sem], tot[sem])
    for t in range(3):
        if known["g"].get("rc%d" % t, 0) < NENG:
            g.wait_ge(T.sem["rc%d" % t], NENG)
